import numpy as np
import ml_dtypes


def mxq(x, axis, fmt="e4m3"):
    dtype, down = {"e4m3": (ml_dtypes.float8_e4m3fn, 7), "e5m2": (ml_dtypes.float8_e5m2, 14)}[fmt]
    v = np.moveaxis(np.asarray(x, np.float32).astype(ml_dtypes.bfloat16).astype(np.float64), axis, -1)
    blocks = v.reshape(v.shape[:-1] + (-1, 32))
    amax = np.abs(blocks).max(-1, keepdims=True)
    byte = np.maximum(np.where(amax > 0, np.frexp(amax)[1] - 1 + 127, 0) - down, 1)
    scale = np.exp2(byte - 127.0)
    codes = (blocks / scale).astype(np.float32).astype(dtype).astype(np.float64)
    return np.moveaxis((codes * scale).reshape(v.shape), -1, axis)


WIDE = False


def mx_kscale(k):
    if not WIDE:
        return np.ones(k)
    levels = np.array([10, -10, 5, -5, 0])
    if k % 512:
        return np.exp2(np.random.permutation(np.resize(levels, k // 32))).repeat(32)
    a = np.empty((k // 512, 16))
    for p in range(k // 512):
        a[p, :8] = np.random.permutation(np.resize(levels, 8))
        for g in range(8):
            far = levels[np.abs(levels - a[p, g]) >= 10]
            a[p, g + 8] = far[np.random.randint(len(far))]
    return np.exp2(a.ravel()).repeat(32)


def f64(x):
    return np.asarray(x).astype(np.float64)


def striped(idx):
    return np.tile(idx.reshape(-1, 16).T, (8, 1)).astype(np.uint16)


def unstriped(offs):
    return offs[:16].T.reshape(-1).astype(np.int64)


E2M1 = np.array([0.0, 0.5, 1.0, 1.5, 2.0, 3.0, 4.0, 6.0, -0.0, -0.5, -1.0, -1.5, -2.0, -3.0, -4.0, -6.0])


def pack_weight(w, fmt):
    k, n = w.shape
    w = f64(np.asarray(w, np.float32).astype(ml_dtypes.bfloat16)).reshape(k // 32, 32, n)
    amax = np.abs(w).max(1)
    if fmt == "e4m3":
        byte = np.frexp(amax)[1] - 1 + 127 - 7
    else:
        mant, ex = np.frexp(amax / 6.0)
        byte = np.where(mant > 0.5, ex, ex - 1) + 127
    byte = np.clip(np.where(amax > 0, byte, 1), 1, 254)
    scaled = (w * np.exp2(127.0 - byte)[:, None, :]).reshape(k, n).astype(np.float32)
    by_word = np.ascontiguousarray(scaled.reshape(k // 512, 128, 4, n).transpose(0, 1, 3, 2))
    if fmt == "e4m3":
        words = by_word.astype(ml_dtypes.float8_e4m3fn).view(np.uint8)
    else:
        c = by_word.astype(ml_dtypes.float4_e2m1fn).view(np.uint8) & 0xF
        words = (c[..., 0::2] | (c[..., 1::2] << 4)).reshape(k // 512, 128, 2 * n)
    return np.ascontiguousarray(words), np.ascontiguousarray(byte.astype(np.uint8).reshape(k // 512, 16, n))


def unpack_weight(words, scales, fmt):
    g, _, n = scales.shape
    words = np.ascontiguousarray(words).reshape(g, 128, n, -1)
    if fmt == "e4m3":
        vals = words.view(ml_dtypes.float8_e4m3fn).astype(np.float64)
    else:
        nib = np.empty((g, 128, n, 4), np.uint8)
        nib[..., 0::2] = words & 0xF
        nib[..., 1::2] = words >> 4
        vals = E2M1[nib]
    vals = vals * np.repeat(np.exp2(scales.astype(np.float64) - 127.0), 8, axis=1)[..., None]
    return vals.transpose(0, 1, 3, 2).reshape(g * 512, n)


def gelu(v):
    return 0.5 * v * (1.0 + np.tanh(np.sqrt(2.0 / np.pi) * (v + 0.044715 * v**3)))


K, T, E, C, H, N = 2048, 512, 4, 256, 512, 512


def by_expert(wq, xq):
    return np.concatenate([wq[e].T @ xq[:, e * C:(e + 1) * C] for e in range(E)], axis=1)


def setup_inputs():
    n = np.random.standard_normal
    s = mx_kscale(K)[:, None]
    u = mx_kscale(H)
    first = np.random.permutation(np.repeat(np.arange(E), T // E))
    second = (first + 1 + np.random.permutation(np.repeat(np.arange(E - 1), -(-T // (E - 1)))[:T])) % E
    while np.bincount(second, minlength=E).max() != T // E:
        load = np.bincount(second, minlength=E); hi, lo = int(load.argmax()), int(load.argmin())
        t = np.flatnonzero((second == hi) & (first != lo))[0]; second[t] = lo
    slot_token = np.empty(E * C, np.int64); pos = np.empty((2, T), np.int64); fill = np.zeros(E, np.int64)
    place = np.stack([np.random.permutation(C) for _ in range(E)])
    for r, deal in enumerate((first, second)):
        for t in np.random.permutation(T):
            e = deal[t]; j = e * C + place[e, fill[e]]; fill[e] += 1; slot_token[j] = t; pos[r, t] = j
    g = np.random.uniform(0.2, 0.8, T)
    w1 = [pack_weight(m, "e2m1") for m in n((E, K, H)) / np.sqrt(K) / s[None] * u[None, None, :]]
    w2 = [pack_weight(m, "e2m1") for m in n((E, H, N)) / np.sqrt(H) / u[None, :, None]]
    x = pack_weight(n((K, T)) * s, "e4m3")
    return {
        "x_words": x[0],
        "x_scales": x[1],
        "w1_words": np.stack([m[0] for m in w1]),
        "w1_scales": np.stack([m[1] for m in w1]),
        "w2_words": np.stack([m[0] for m in w2]),
        "w2_scales": np.stack([m[1] for m in w2]),
        "gate": np.stack([np.tile(g, (N, 1)), np.tile(1.0 - g, (N, 1))]).astype(np.float32),
        "offs": striped(slot_token),
        "pos1": striped(pos[0]),
        "pos2": striped(pos[1]),
    }


def reference(x_words, x_scales, w1_words, w1_scales, w2_words, w2_scales, gate, offs, pos1, pos2):
    idx = unstriped(offs)
    w1 = np.stack([unpack_weight(w1_words[e], w1_scales[e], "e2m1") for e in range(E)])
    w2 = np.stack([unpack_weight(w2_words[e], w2_scales[e], "e2m1") for e in range(E)])
    xq = unpack_weight(x_words, x_scales, "e4m3")[:, idx]
    h = gelu(by_expert(w1, xq))
    y = by_expert(w2, mxq(h, 0, "e4m3"))
    return f64(gate[0]) * y[:, unstriped(pos1)] + f64(gate[1]) * y[:, unstriped(pos2)]

@@ -1,0 +1,233 @@
+from contextlib import ExitStack
+
+import concourse.mybir as mybir
+from concourse.masks import make_identity
+
+K, T, E, C, H, N = 2048, 512, 4, 256, 512, 512
+SLOTS = E * C
+FLOPS = 2 * SLOTS * (K * H + H * N)
+
+F32 = mybir.dt.float32
+BF16 = mybir.dt.bfloat16
+I32 = mybir.dt.int32
+U32 = mybir.dt.uint32
+U16 = mybir.dt.uint16
+U8 = mybir.dt.uint8
+FP8X4 = mybir.dt.float8_e4m3fn_x4
+FP4X4 = mybir.dt.float4_e2m1fn_x4
+GELU = mybir.ActivationFunctionType.Gelu_apprx_tanh
+MULT = mybir.AluOpType.mult
+ADD = mybir.AluOpType.add
+
+P = 128
+PASSES = K // 512
+BLOCKS = C // P
+N_TILES = N // P
+PER_COL = 16
+SHIFT_ROWS = 112
+
+
+def tile_moe_pkd_mlp_gelu_kernel(tc, x_words, x_scales, w1_words, w1_scales, w2_words, w2_scales, gate, offs, pos1, pos2, out):
+    nc = tc.nc
+    with ExitStack() as ctx:
+        keep = ctx.enter_context(tc.tile_pool(name="keep", bufs=1))
+        ring = ctx.enter_context(tc.tile_pool(name="ring", bufs=3))
+        weights = ctx.enter_context(tc.tile_pool(name="weights", bufs=2))
+        psum_a = ctx.enter_context(tc.psum_pool(name="psum_a", bufs=4))
+        psum_t = ctx.enter_context(tc.psum_pool(name="psum_t", bufs=2))
+        psum_y = ctx.enter_context(tc.psum_pool(name="psum_y", bufs=2))
+
+        offs_t = keep.tile([P, SLOTS // PER_COL], U16, name="offs_t")
+        pos1_t = keep.tile([P, T // PER_COL], U16, name="pos1_t")
+        pos2_t = keep.tile([P, T // PER_COL], U16, name="pos2_t")
+        x_scale_rows = keep.tile([P, T], U8, name="x_scale_rows", align_bytes=64)
+        x_halves = [keep.tile([P, 2 * T], I32, name="x_half%d" % i, align_bytes=64) for i in range(2)]
+        groups = [(0, 1), (1, E)]
+        w1_planes = [keep.tile([P, (hi - lo) * PASSES * H], U8, name="w1_planes%d" % lo, align_bytes=64) for lo, hi in groups]
+        slot_scales = [keep.tile([P, (hi - lo) * C], U8, name="slot_scales%d" % lo, align_bytes=64) for lo, hi in groups]
+        shifted = [keep.tile([P, (PASSES - 1) * (hi - lo) * C], U8, name="shifted%d" % lo, align_bytes=64) for lo, hi in groups]
+        w2_planes = w1_planes[0]
+        ident = keep.tile([P, P], F32, name="ident")
+        slot_words = [[keep.tile([P, C], U32, name="slot_words%d_%d" % (e, a), tag="slot_words%d_%d" % (e, a), align_bytes=64) for a in range(PASSES)] for e in range(E)]
+        h_codes = [keep.tile([P, C], U32, name="h_codes%d" % e, align_bytes=64) for e in range(E)]
+        h_scales = [keep.tile([P, C], U8, name="h_scales%d" % e, align_bytes=64) for e in range(E)]
+        y_rows = [keep.tile([P, SLOTS], F32, name="y_rows%d" % j) for j in range(N_TILES)]
+
+        def zero(engine, tile):
+            engine.memset(tile[:].bitcast(I32), 0)
+
+        def load_planes(tile, rows):
+            planes = rows.shape[0]
+            by_r = rows.bitcast(I32).rearrange("s (q r) c -> r q s c", r=4)
+            for r in range(4):
+                nc.sync.dma_start(tile[r:P:32, :].bitcast(I32).rearrange("q (s c) -> q s c", s=planes), by_r[r])
+
+        def load_codes(words):
+            tile = weights.tile([P, PASSES * 2 * H], U8, name="codes", align_bytes=64)
+            nc.sync.dma_start(tile[:].bitcast(I32).rearrange("p (s c) -> p s c", s=words.shape[0]), words.bitcast(I32).rearrange("s p c -> p s c"))
+            return tile
+
+        def load_x_half(i):
+            words = x_words[2 * i : 2 * i + 2].rearrange("a p t r -> a p (t r)").bitcast(I32)
+            nc.sync.dma_start(x_halves[i][:].rearrange("p (a t) -> p a t", a=2), words.rearrange("a p t -> p a t"))
+
+        zero(nc.vector, x_scale_rows)
+        zero(nc.vector, w1_planes[0])
+        warm = keep.tile([P, 1], F32, name="warm")
+        nc.vector.memset(warm[:], 0.0)
+        nc.scalar.activation(warm[:], warm[:], GELU)
+        zero(nc.vector, shifted[0])
+        zero(nc.gpsimd, w1_planes[1])
+        zero(nc.vector, shifted[1])
+        make_identity(nc, ident[:])
+
+        nc.sync.dma_start(offs_t[:], offs)
+        nc.sync.dma_start(pos1_t[:], pos1)
+        nc.sync.dma_start(pos2_t[:], pos2)
+        for q in range(4):
+            nc.sync.dma_start(x_scale_rows[32 * q : 32 * q + 16, :].bitcast(I32), x_scales[:, 4 * q : 4 * q + 4, :].bitcast(I32))
+        load_x_half(0)
+        load_planes(w1_planes[0], w1_scales[0])
+        w1_codes = [load_codes(w1_words[0])]
+        load_x_half(1)
+        load_planes(w1_planes[1], w1_scales[1:E].rearrange("e s f c -> (e s) f c"))
+        w1_codes.append(load_codes(w1_words[1]))
+
+        def gather_scales(g):
+            lo, hi = groups[g]
+            width = (hi - lo) * C
+            for e in range(lo, hi):
+                entries = offs_t[:, e * C // PER_COL : (e + 1) * C // PER_COL]
+                nc.vector.tensor_copy(slot_scales[g][:, (e - lo) * C : (e - lo + 1) * C], x_scale_rows[:].indirect(entries))
+            for a in range(1, PASSES):
+                nc.scalar.dma_start(
+                    shifted[g][0:SHIFT_ROWS, (a - 1) * width : a * width].bitcast(I32),
+                    slot_scales[g][4 * a : 4 * a + SHIFT_ROWS, :].bitcast(I32),
+                )
+
+        def gather_words(e):
+            entries = offs_t[:, e * C // PER_COL : (e + 1) * C // PER_COL]
+            for a in range(PASSES):
+                window = x_halves[a // 2][:, (a % 2) * T : (a % 2 + 1) * T].bitcast(U32)
+                nc.vector.tensor_copy(slot_words[e][a][:], window.indirect(entries))
+
+        def token_plane(e, a, b):
+            g = min(e, 1)
+            lo, hi = groups[g]
+            first = (e - lo) * C + b * P
+            if a == 0:
+                return slot_scales[g][:, first : first + P]
+            first = first + (a - 1) * (hi - lo) * C
+            return shifted[g][:, first : first + P]
+
+        pre = {}
+
+        def first_layer(e):
+            g = min(e, 1)
+            lo = groups[g][0]
+            for b in range(BLOCKS):
+                pre[e, b] = psum_a.tile([P, H], F32, name="acc")
+            steps = [(a, b) for b in range(BLOCKS) for a in range(PASSES)]
+            if e == 0:
+                steps = sorted(steps)
+            for a, b in steps:
+                plane = ((e - lo) * PASSES + a) * H
+                nc.tensor.matmul_mx(
+                    out=pre[e, b][:],
+                    lhsT=slot_words[e][a][:, b * P : (b + 1) * P].bitcast(FP8X4),
+                    lhsT_scale=token_plane(e, a, b),
+                    rhs=w1_codes[e][:, a * 2 * H : (a + 1) * 2 * H].bitcast(FP4X4),
+                    rhs_scale=w1_planes[g][:, plane : plane + H],
+                    start=(a == 0),
+                    stop=(a == PASSES - 1),
+                )
+
+        def hidden(e):
+            for b in range(BLOCKS):
+                h_slots = ring.tile([P, H], BF16, name="h_slots")
+                nc.scalar.activation(
+                    h_slots[:].rearrange("s (u p d) -> s u p d", u=2, d=2),
+                    pre[e, b][:].rearrange("s (p u d) -> s u p d", u=2, d=2),
+                    GELU,
+                )
+                pairs = h_slots[:].bitcast(F32)
+                turned = psum_t.tile([P, 2 * P], F32, name="turned")
+                for u in range(2):
+                    nc.tensor.transpose(turned[:, u * P : (u + 1) * P], pairs[:, u * P : (u + 1) * P], ident[:])
+                h_grouped = ring.tile([P, 4 * P], BF16, name="h_grouped", align_bytes=64, bufs=E * BLOCKS)
+                copy = nc.vector.tensor_copy if e == E - 1 else nc.scalar.copy
+                copy(
+                    h_grouped[:].bitcast(F32).rearrange("p (s u) -> p s u", u=2),
+                    turned[:].rearrange("p (u s) -> p s u", u=2),
+                )
+                nc.vector.quantize_mx(
+                    out=h_codes[e][:, b * P : (b + 1) * P].bitcast(FP8X4),
+                    scales=h_scales[e][:, b * P : (b + 1) * P],
+                    in_=h_grouped[:],
+                )
+
+        def second_layer(j, first_slot, n_slots, copy):
+            sums = psum_y.tile([P, n_slots], F32, name="sums")
+            width = min(C, n_slots)
+            for i in range(0, n_slots, width):
+                e, c = divmod(first_slot + i, C)
+                col = e * N + j * P
+                nc.tensor.matmul_mx(
+                    out=sums[:, i : i + width],
+                    lhsT=w2_codes[:, 2 * col : 2 * (col + P)].bitcast(FP4X4),
+                    lhsT_scale=w2_planes[:, col : col + P],
+                    rhs=h_codes[e][:, c : c + width].bitcast(FP8X4),
+                    rhs_scale=h_scales[e][:, c : c + width],
+                    start=True,
+                    stop=True,
+                )
+            copy(y_rows[j][:, first_slot : first_slot + n_slots], sums[:])
+
+        gather_scales(0)
+        gather_words(0)
+        gather_scales(1)
+        for e in range(E):
+            if e > 0:
+                gather_words(e)
+            first_layer(e)
+            if e + 2 < E:
+                w1_codes.append(load_codes(w1_words[e + 2]))
+            if e == 0:
+                load_planes(w2_planes, w2_scales.rearrange("e s f c -> (e s) f c"))
+            if e == 1:
+                gates = keep.tile([P, 2 * T], F32, name="gates", tag="slot_words1_3", align_bytes=64)
+                nc.sync.dma_start(gates[:].rearrange("p (r t) -> p r t", r=2), gate[:, 0:P, :].rearrange("r p t -> p r t"))
+            if e == 2:
+                w2_codes = load_codes(w2_words.rearrange("e s p c -> (e s) p c"))
+            if e > 0:
+                hidden(e - 1)
+        hidden(E - 1)
+        second_layer(0, 0, 2 * C, nc.vector.tensor_copy)
+        second_layer(0, 2 * C, C, nc.vector.tensor_copy)
+        second_layer(0, 3 * C, P, nc.scalar.copy)
+        second_layer(0, 3 * C + P, P, nc.scalar.copy)
+        for j in range(1, N_TILES):
+            second_layer(j, 0, 2 * C, nc.scalar.copy)
+            second_layer(j, 2 * C, 2 * C, nc.scalar.copy)
+
+        pieces = [(j, 0, T) for j in range(N_TILES - 1)] + [(N_TILES - 1, 0, T // 2), (N_TILES - 1, T // 2, T)]
+        products = {}
+
+        def product(piece, r):
+            j, lo, hi = piece
+            entries = (pos1_t, pos2_t)[r][:, lo // PER_COL : hi // PER_COL]
+            products[piece, r] = ring.tile([P, hi - lo], F32, name="product%d" % r)
+            nc.vector.tensor_tensor(products[piece, r][:], y_rows[j][:].indirect(entries), gates[:, r * T + lo : r * T + hi], MULT)
+
+        def finish(piece):
+            j, lo, hi = piece
+            total = ring.tile([P, hi - lo], F32, name="total")
+            nc.vector.tensor_tensor(total[:], products[piece, 0][:], products[piece, 1][:], ADD)
+            nc.sync.dma_start(out[j * P : (j + 1) * P, lo:hi], total[:])
+
+        for i, piece in enumerate(pieces):
+            product(piece, 0)
+            if i > 0:
+                finish(pieces[i - 1])
+            product(piece, 1)
+        finish(pieces[-1])

@@ -32,7 +32,6 @@ def tile_moe_pkd_mlp_gelu_kernel(tc, x_words, x_scales, w1_words, w1_scales, w2_
     with ExitStack() as ctx:
         keep = ctx.enter_context(tc.tile_pool(name="keep", bufs=1))
         ring = ctx.enter_context(tc.tile_pool(name="ring", bufs=3))
-        weights = ctx.enter_context(tc.tile_pool(name="weights", bufs=2))
         psum_a = ctx.enter_context(tc.psum_pool(name="psum_a", bufs=4))
         psum_t = ctx.enter_context(tc.psum_pool(name="psum_t", bufs=2))
         psum_y = ctx.enter_context(tc.psum_pool(name="psum_y", bufs=2))
@@ -40,8 +39,8 @@ def tile_moe_pkd_mlp_gelu_kernel(tc, x_words, x_scales, w1_words, w1_scales, w2_
         offs_t = keep.tile([P, SLOTS // PER_COL], U16, name="offs_t")
         pos1_t = keep.tile([P, T // PER_COL], U16, name="pos1_t")
         pos2_t = keep.tile([P, T // PER_COL], U16, name="pos2_t")
-        x_scale_rows = keep.tile([P, T], U8, name="x_scale_rows", align_bytes=64)
-        x_halves = [keep.tile([P, 2 * T], I32, name="x_half%d" % i, align_bytes=64) for i in range(2)]
+        x_scale_rows = keep.tile([P, T], U8, name="x_scale_rows", tag="early", align_bytes=64)
+        x_codes = keep.tile([P, PASSES * T], I32, name="x_codes", align_bytes=64)
         groups = [(0, 1), (1, E)]
         w1_planes = [keep.tile([P, (hi - lo) * PASSES * H], U8, name="w1_planes%d" % lo, align_bytes=64) for lo, hi in groups]
         slot_scales = [keep.tile([P, (hi - lo) * C], U8, name="slot_scales%d" % lo, align_bytes=64) for lo, hi in groups]
@@ -56,29 +55,29 @@ def tile_moe_pkd_mlp_gelu_kernel(tc, x_words, x_scales, w1_words, w1_scales, w2_
         def zero(engine, tile):
             engine.memset(tile[:].bitcast(I32), 0)
 
-        def load_planes(tile, rows):
+        def load_planes(queue, tile, rows):
             planes = rows.shape[0]
             by_r = rows.bitcast(I32).rearrange("s (q r) c -> r q s c", r=4)
             for r in range(4):
-                nc.sync.dma_start(tile[r:P:32, :].bitcast(I32).rearrange("q (s c) -> q s c", s=planes), by_r[r])
+                queue.dma_start(tile[r:P:32, :].bitcast(I32).rearrange("q (s c) -> q s c", s=planes), by_r[r])
 
-        def load_codes(words):
-            tile = weights.tile([P, PASSES * 2 * H], U8, name="codes", align_bytes=64)
+        def load_codes(tile, words):
             nc.sync.dma_start(tile[:].bitcast(I32).rearrange("p (s c) -> p s c", s=words.shape[0]), words.bitcast(I32).rearrange("s p c -> p s c"))
-            return tile
 
-        def load_x_half(i):
-            words = x_words[2 * i : 2 * i + 2].rearrange("a p t r -> a p (t r)").bitcast(I32)
-            nc.sync.dma_start(x_halves[i][:].rearrange("p (a t) -> p a t", a=2), words.rearrange("a p t -> p a t"))
+        w1_codes = {}
+
+        def load_w1(e, passes, tag):
+            tile = keep.tile([P, len(passes) * 2 * H], U8, name="w1_codes", tag=tag, align_bytes=64)
+            load_codes(tile, w1_words[e, passes[0] : passes[-1] + 1])
+            for i, a in enumerate(passes):
+                w1_codes[e, a] = tile[:, i * 2 * H : (i + 1) * 2 * H]
 
         zero(nc.vector, x_scale_rows)
         zero(nc.vector, w1_planes[0])
-        warm = keep.tile([P, 1], F32, name="warm")
-        nc.vector.memset(warm[:], 0.0)
-        nc.scalar.activation(warm[:], warm[:], GELU)
         zero(nc.vector, shifted[0])
         zero(nc.gpsimd, w1_planes[1])
         zero(nc.vector, shifted[1])
+        load_planes(nc.gpsimd, w1_planes[1], w1_scales[1:E].rearrange("e s f c -> (e s) f c"))
         make_identity(nc, ident[:])
 
         nc.sync.dma_start(offs_t[:], offs)
@@ -86,21 +85,24 @@ def tile_moe_pkd_mlp_gelu_kernel(tc, x_words, x_scales, w1_words, w1_scales, w2_
         nc.sync.dma_start(pos2_t[:], pos2)
         for q in range(4):
             nc.sync.dma_start(x_scale_rows[32 * q : 32 * q + 16, :].bitcast(I32), x_scales[:, 4 * q : 4 * q + 4, :].bitcast(I32))
-        load_x_half(0)
-        load_planes(w1_planes[0], w1_scales[0])
-        w1_codes = [load_codes(w1_words[0])]
-        load_x_half(1)
-        load_planes(w1_planes[1], w1_scales[1:E].rearrange("e s f c -> (e s) f c"))
-        w1_codes.append(load_codes(w1_words[1]))
+        nc.sync.dma_start(
+            x_codes[:].rearrange("p (a t) -> p a t", a=PASSES),
+            x_words.rearrange("a p t r -> a p (t r)").bitcast(I32).rearrange("a p t -> p a t"),
+        )
+        load_w1(0, range(PASSES), "w1_first")
+        load_planes(nc.sync, w1_planes[0], w1_scales[0])
 
         def gather_scales(g):
             lo, hi = groups[g]
-            width = (hi - lo) * C
             for e in range(lo, hi):
                 entries = offs_t[:, e * C // PER_COL : (e + 1) * C // PER_COL]
                 nc.vector.tensor_copy(slot_scales[g][:, (e - lo) * C : (e - lo + 1) * C], x_scale_rows[:].indirect(entries))
+
+        def shift_scales(g):
+            lo, hi = groups[g]
+            width = (hi - lo) * C
             for a in range(1, PASSES):
-                nc.scalar.dma_start(
+                (nc.scalar, nc.sync)[g].dma_start(
                     shifted[g][0:SHIFT_ROWS, (a - 1) * width : a * width].bitcast(I32),
                     slot_scales[g][4 * a : 4 * a + SHIFT_ROWS, :].bitcast(I32),
                 )
@@ -108,7 +110,7 @@ def tile_moe_pkd_mlp_gelu_kernel(tc, x_words, x_scales, w1_words, w1_scales, w2_
         def gather_words(e):
             entries = offs_t[:, e * C // PER_COL : (e + 1) * C // PER_COL]
             for a in range(PASSES):
-                window = x_halves[a // 2][:, (a % 2) * T : (a % 2 + 1) * T].bitcast(U32)
+                window = x_codes[:, a * T : (a + 1) * T].bitcast(U32)
                 nc.vector.tensor_copy(slot_words[e][a][:], window.indirect(entries))
 
         def token_plane(e, a, b):
@@ -122,13 +124,13 @@ def tile_moe_pkd_mlp_gelu_kernel(tc, x_words, x_scales, w1_words, w1_scales, w2_
 
         pre = {}
 
-        def first_layer(e):
+        def first_layer(e, blocks):
             g = min(e, 1)
             lo = groups[g][0]
-            for b in range(BLOCKS):
+            for b in blocks:
                 pre[e, b] = psum_a.tile([P, H], F32, name="acc")
-            steps = [(a, b) for b in range(BLOCKS) for a in range(PASSES)]
-            if e == 0:
+            steps = [(a, b) for b in blocks for a in range(PASSES)]
+            if e < 2:
                 steps = sorted(steps)
             for a, b in steps:
                 plane = ((e - lo) * PASSES + a) * H
@@ -136,7 +138,7 @@ def tile_moe_pkd_mlp_gelu_kernel(tc, x_words, x_scales, w1_words, w1_scales, w2_
                     out=pre[e, b][:],
                     lhsT=slot_words[e][a][:, b * P : (b + 1) * P].bitcast(FP8X4),
                     lhsT_scale=token_plane(e, a, b),
-                    rhs=w1_codes[e][:, a * 2 * H : (a + 1) * 2 * H].bitcast(FP4X4),
+                    rhs=w1_codes[e, a].bitcast(FP4X4),
                     rhs_scale=w1_planes[g][:, plane : plane + H],
                     start=(a == 0),
                     stop=(a == PASSES - 1),
@@ -184,26 +186,33 @@ def tile_moe_pkd_mlp_gelu_kernel(tc, x_words, x_scales, w1_words, w1_scales, w2_
             copy(y_rows[j][:, first_slot : first_slot + n_slots], sums[:])
 
         gather_scales(0)
-        gather_words(0)
+        shift_scales(0)
         gather_scales(1)
-        for e in range(E):
+        load_w1(1, range(PASSES), "early")
+        shift_scales(1)
+        gather_words(0)
+        for e in range(E - 1):
             if e > 0:
                 gather_words(e)
-            first_layer(e)
+            first_layer(e, range(BLOCKS))
             if e + 2 < E:
-                w1_codes.append(load_codes(w1_words[e + 2]))
+                load_w1(e + 2, range(PASSES), ("slot_words0_0", "slot_words1_0")[e])
             if e == 0:
-                load_planes(w2_planes, w2_scales.rearrange("e s f c -> (e s) f c"))
+                load_planes(nc.sync, w2_planes, w2_scales.rearrange("e s f c -> (e s) f c"))
+                w2_codes = keep.tile([P, E * 2 * N], U8, name="w2_codes", tag="slot_words0_3", align_bytes=64)
+                load_codes(w2_codes, w2_words.rearrange("e s p c -> (e s) p c"))
             if e == 1:
                 gates = keep.tile([P, 2 * T], F32, name="gates", tag="slot_words1_3", align_bytes=64)
                 nc.sync.dma_start(gates[:].rearrange("p (r t) -> p r t", r=2), gate[:, 0:P, :].rearrange("r p t -> p r t"))
-            if e == 2:
-                w2_codes = load_codes(w2_words.rearrange("e s p c -> (e s) p c"))
             if e > 0:
                 hidden(e - 1)
-        hidden(E - 1)
+        gather_words(E - 1)
+        first_layer(E - 1, [0])
+        hidden(E - 2)
         second_layer(0, 0, 2 * C, nc.vector.tensor_copy)
+        first_layer(E - 1, [1])
         second_layer(0, 2 * C, C, nc.vector.tensor_copy)
+        hidden(E - 1)
         second_layer(0, 3 * C, P, nc.scalar.copy)
         second_layer(0, 3 * C + P, P, nc.scalar.copy)
         for j in range(1, N_TILES):
@@ -222,7 +231,19 @@ def tile_moe_pkd_mlp_gelu_kernel(tc, x_words, x_scales, w1_words, w1_scales, w2_
         def finish(piece):
             j, lo, hi = piece
             total = ring.tile([P, hi - lo], F32, name="total")
-            nc.vector.tensor_tensor(total[:], products[piece, 0][:], products[piece, 1][:], ADD)
+            if j == N_TILES - 1:
+                nc.vector.tensor_tensor(total[:], products[piece, 0][:], products[piece, 1][:], ADD)
+            else:
+                by_token = psum_a.tile([P, T], F32, name="acc")
+                for c in range(0, T, P):
+                    for r in range(2):
+                        nc.tensor.matmul(by_token[:, c : c + P], lhsT=products[piece, r][:, c : c + P], rhs=ident[:], is_transpose=True, start=(r == 0), stop=(r == 1))
+                staged = ring.tile([P, T], F32, name="staged")
+                nc.scalar.copy(staged[:], by_token[:])
+                by_row = psum_a.tile([P, T], F32, name="acc")
+                for c in range(0, T, P):
+                    nc.tensor.transpose(by_row[:, c : c + P], staged[:, c : c + P], ident[:])
+                nc.scalar.copy(total[:], by_row[:])
             nc.sync.dma_start(out[j * P : (j + 1) * P, lo:hi], total[:])
 
         for i, piece in enumerate(pieces):

@@ -42,10 +42,9 @@ def tile_moe_pkd_mlp_gelu_kernel(tc, x_words, x_scales, w1_words, w1_scales, w2_
         x_scale_rows = keep.tile([P, T], U8, name="x_scale_rows", tag="early", align_bytes=64)
         x_codes = keep.tile([P, PASSES * T], I32, name="x_codes", align_bytes=64)
         groups = [(0, 1), (1, E)]
-        w1_planes = [keep.tile([P, (hi - lo) * PASSES * H], U8, name="w1_planes%d" % lo, align_bytes=64) for lo, hi in groups]
+        w1_planes = [keep.tile([P, 2 * PASSES * H], U8, name="w1_planes", align_bytes=64)]
         slot_scales = [keep.tile([P, (hi - lo) * C], U8, name="slot_scales%d" % lo, align_bytes=64) for lo, hi in groups]
-        shifted = [keep.tile([P, (PASSES - 1) * (hi - lo) * C], U8, name="shifted%d" % lo, align_bytes=64) for lo, hi in groups]
-        w2_planes = w1_planes[0]
+        shifted = [[keep.tile([P, (hi - lo) * C], U8, name="shifted%d_%d" % (lo, a), align_bytes=64) for a in range(1, PASSES)] for lo, hi in groups]
         ident = keep.tile([P, P], F32, name="ident")
         slot_words = [[keep.tile([P, C], U32, name="slot_words%d_%d" % (e, a), tag="slot_words%d_%d" % (e, a), align_bytes=64) for a in range(PASSES)] for e in range(E)]
         h_codes = [keep.tile([P, C], U32, name="h_codes%d" % e, align_bytes=64) for e in range(E)]
@@ -55,11 +54,11 @@ def tile_moe_pkd_mlp_gelu_kernel(tc, x_words, x_scales, w1_words, w1_scales, w2_
         def zero(engine, tile):
             engine.memset(tile[:].bitcast(I32), 0)
 
-        def load_planes(queue, tile, rows):
+        def load_planes(tile, rows):
             planes = rows.shape[0]
             by_r = rows.bitcast(I32).rearrange("s (q r) c -> r q s c", r=4)
             for r in range(4):
-                queue.dma_start(tile[r:P:32, :].bitcast(I32).rearrange("q (s c) -> q s c", s=planes), by_r[r])
+                nc.sync.dma_start(tile[r:P:32, :].bitcast(I32).rearrange("q (s c) -> q s c", s=planes), by_r[r])
 
         def load_codes(tile, words):
             nc.sync.dma_start(tile[:].bitcast(I32).rearrange("p (s c) -> p s c", s=words.shape[0]), words.bitcast(I32).rearrange("s p c -> p s c"))
@@ -74,10 +73,9 @@ def tile_moe_pkd_mlp_gelu_kernel(tc, x_words, x_scales, w1_words, w1_scales, w2_
 
         zero(nc.vector, x_scale_rows)
         zero(nc.vector, w1_planes[0])
-        zero(nc.vector, shifted[0])
-        zero(nc.gpsimd, w1_planes[1])
-        zero(nc.vector, shifted[1])
-        load_planes(nc.gpsimd, w1_planes[1], w1_scales[1:E].rearrange("e s f c -> (e s) f c"))
+        for group in shifted:
+            for tile in group:
+                zero(nc.gpsimd, tile)
         make_identity(nc, ident[:])
 
         nc.sync.dma_start(offs_t[:], offs)
@@ -90,7 +88,7 @@ def tile_moe_pkd_mlp_gelu_kernel(tc, x_words, x_scales, w1_words, w1_scales, w2_
             x_words.rearrange("a p t r -> a p (t r)").bitcast(I32).rearrange("a p t -> p a t"),
         )
         load_w1(0, range(PASSES), "w1_first")
-        load_planes(nc.sync, w1_planes[0], w1_scales[0])
+        load_planes(w1_planes[0], w1_scales[0:2].rearrange("e s f c -> (e s) f c"))
 
         def gather_scales(g):
             lo, hi = groups[g]
@@ -99,11 +97,9 @@ def tile_moe_pkd_mlp_gelu_kernel(tc, x_words, x_scales, w1_words, w1_scales, w2_
                 nc.vector.tensor_copy(slot_scales[g][:, (e - lo) * C : (e - lo + 1) * C], x_scale_rows[:].indirect(entries))
 
         def shift_scales(g):
-            lo, hi = groups[g]
-            width = (hi - lo) * C
             for a in range(1, PASSES):
-                (nc.scalar, nc.sync)[g].dma_start(
-                    shifted[g][0:SHIFT_ROWS, (a - 1) * width : a * width].bitcast(I32),
+                nc.sync.dma_start(
+                    shifted[g][a - 1][0:SHIFT_ROWS, :].bitcast(I32),
                     slot_scales[g][4 * a : 4 * a + SHIFT_ROWS, :].bitcast(I32),
                 )
 
@@ -119,27 +115,24 @@ def tile_moe_pkd_mlp_gelu_kernel(tc, x_words, x_scales, w1_words, w1_scales, w2_
             first = (e - lo) * C + b * P
             if a == 0:
                 return slot_scales[g][:, first : first + P]
-            first = first + (a - 1) * (hi - lo) * C
-            return shifted[g][:, first : first + P]
+            return shifted[g][a - 1][:, first : first + P]
 
         pre = {}
 
         def first_layer(e, blocks):
-            g = min(e, 1)
-            lo = groups[g][0]
             for b in blocks:
                 pre[e, b] = psum_a.tile([P, H], F32, name="acc")
             steps = [(a, b) for b in blocks for a in range(PASSES)]
             if e < 2:
                 steps = sorted(steps)
             for a, b in steps:
-                plane = ((e - lo) * PASSES + a) * H
+                plane = ((e % 2) * PASSES + a) * H
                 nc.tensor.matmul_mx(
                     out=pre[e, b][:],
                     lhsT=slot_words[e][a][:, b * P : (b + 1) * P].bitcast(FP8X4),
                     lhsT_scale=token_plane(e, a, b),
                     rhs=w1_codes[e, a].bitcast(FP4X4),
-                    rhs_scale=w1_planes[g][:, plane : plane + H],
+                    rhs_scale=w1_planes[e // 2][:, plane : plane + H],
                     start=(a == 0),
                     stop=(a == PASSES - 1),
                 )
@@ -157,7 +150,7 @@ def tile_moe_pkd_mlp_gelu_kernel(tc, x_words, x_scales, w1_words, w1_scales, w2_
                 for u in range(2):
                     nc.tensor.transpose(turned[:, u * P : (u + 1) * P], pairs[:, u * P : (u + 1) * P], ident[:])
                 h_grouped = ring.tile([P, 4 * P], BF16, name="h_grouped", align_bytes=64, bufs=E * BLOCKS)
-                copy = nc.vector.tensor_copy if e == E - 1 else nc.scalar.copy
+                copy = nc.vector.tensor_copy if (e, b) == (E - 1, 0) else nc.scalar.copy
                 copy(
                     h_grouped[:].bitcast(F32).rearrange("p (s u) -> p s u", u=2),
                     turned[:].rearrange("p (u s) -> p s u", u=2),
@@ -169,7 +162,7 @@ def tile_moe_pkd_mlp_gelu_kernel(tc, x_words, x_scales, w1_words, w1_scales, w2_
                 )
 
         def second_layer(j, first_slot, n_slots, copy):
-            sums = psum_y.tile([P, n_slots], F32, name="sums")
+            sums = psum_y.tile([P, n_slots], F32, name="sums") if j < 2 else psum_a.tile([P, n_slots], F32, name="acc")
             width = min(C, n_slots)
             for i in range(0, n_slots, width):
                 e, c = divmod(first_slot + i, C)
@@ -195,13 +188,18 @@ def tile_moe_pkd_mlp_gelu_kernel(tc, x_words, x_scales, w1_words, w1_scales, w2_
             if e > 0:
                 gather_words(e)
             first_layer(e, range(BLOCKS))
-            if e + 2 < E:
-                load_w1(e + 2, range(PASSES), ("slot_words0_0", "slot_words1_0")[e])
             if e == 0:
-                load_planes(nc.sync, w2_planes, w2_scales.rearrange("e s f c -> (e s) f c"))
+                load_w1(2, range(PASSES), "slot_words0_0")
+                w1_planes.append(keep.tile([P, 2 * PASSES * H], U8, name="w1_planes_late", tag="slot_words0_1", align_bytes=64))
+                zero(nc.gpsimd, w1_planes[1])
+                load_planes(w1_planes[1], w1_scales[2:E].rearrange("e s f c -> (e s) f c"))
+                load_w1(3, range(PASSES), "slot_words0_2")
                 w2_codes = keep.tile([P, E * 2 * N], U8, name="w2_codes", tag="slot_words0_3", align_bytes=64)
                 load_codes(w2_codes, w2_words.rearrange("e s p c -> (e s) p c"))
             if e == 1:
+                w2_planes = keep.tile([P, E * N], U8, name="w2_planes", tag="slot_words1_0", align_bytes=64)
+                zero(nc.gpsimd, w2_planes)
+                load_planes(w2_planes, w2_scales.rearrange("e s f c -> (e s) f c"))
                 gates = keep.tile([P, 2 * T], F32, name="gates", tag="slot_words1_3", align_bytes=64)
                 nc.sync.dma_start(gates[:].rearrange("p (r t) -> p r t", r=2), gate[:, 0:P, :].rearrange("r p t -> p r t"))
             if e > 0:
@@ -231,7 +229,7 @@ def tile_moe_pkd_mlp_gelu_kernel(tc, x_words, x_scales, w1_words, w1_scales, w2_
         def finish(piece):
             j, lo, hi = piece
             total = ring.tile([P, hi - lo], F32, name="total")
-            if j == N_TILES - 1:
+            if j >= 2:
                 nc.vector.tensor_tensor(total[:], products[piece, 0][:], products[piece, 1][:], ADD)
             else:
                 by_token = psum_a.tile([P, T], F32, name="acc")

from contextlib import ExitStack

import concourse.mybir as mybir
from concourse.masks import make_identity

K, T, E, C, H, N = 2048, 512, 4, 256, 512, 512
SLOTS = E * C
FLOPS = 2 * SLOTS * (K * H + H * N)

F32 = mybir.dt.float32
BF16 = mybir.dt.bfloat16
I32 = mybir.dt.int32
U32 = mybir.dt.uint32
U16 = mybir.dt.uint16
U8 = mybir.dt.uint8
FP8X4 = mybir.dt.float8_e4m3fn_x4
FP4X4 = mybir.dt.float4_e2m1fn_x4
GELU = mybir.ActivationFunctionType.Gelu_apprx_tanh
MULT = mybir.AluOpType.mult
ADD = mybir.AluOpType.add

P = 128
PASSES = K // 512
BLOCKS = C // P
N_TILES = N // P
PER_COL = 16
SHIFT_ROWS = 112


def tile_moe_pkd_mlp_gelu_kernel(tc, x_words, x_scales, w1_words, w1_scales, w2_words, w2_scales, gate, offs, pos1, pos2, out):
    nc = tc.nc
    with ExitStack() as ctx:
        keep = ctx.enter_context(tc.tile_pool(name="keep", bufs=1))
        ring = ctx.enter_context(tc.tile_pool(name="ring", bufs=3))
        psum_a = ctx.enter_context(tc.psum_pool(name="psum_a", bufs=4))
        psum_t = ctx.enter_context(tc.psum_pool(name="psum_t", bufs=2))
        psum_y = ctx.enter_context(tc.psum_pool(name="psum_y", bufs=2))

        offs_t = keep.tile([P, SLOTS // PER_COL], U16, name="offs_t")
        pos1_t = keep.tile([P, T // PER_COL], U16, name="pos1_t")
        pos2_t = keep.tile([P, T // PER_COL], U16, name="pos2_t")
        x_scale_rows = keep.tile([P, T], U8, name="x_scale_rows", tag="early", align_bytes=64)
        x_codes = keep.tile([P, PASSES * T], I32, name="x_codes", align_bytes=64)
        groups = [(0, 1), (1, E)]
        w1_planes = [keep.tile([P, 2 * PASSES * H], U8, name="w1_planes", align_bytes=64)]
        slot_scales = [keep.tile([P, (hi - lo) * C], U8, name="slot_scales%d" % lo, align_bytes=64) for lo, hi in groups]
        shifted = [[keep.tile([P, (hi - lo) * C], U8, name="shifted%d_%d" % (lo, a), align_bytes=64) for a in range(1, PASSES)] for lo, hi in groups]
        ident = keep.tile([P, P], F32, name="ident")
        slot_words = [[keep.tile([P, C], U32, name="slot_words%d_%d" % (e, a), tag="slot_words%d_%d" % (e, a), align_bytes=64) for a in range(PASSES)] for e in range(E)]
        h_codes = [keep.tile([P, C], U32, name="h_codes%d" % e, align_bytes=64) for e in range(E)]
        h_scales = [keep.tile([P, C], U8, name="h_scales%d" % e, align_bytes=64) for e in range(E)]
        y_rows = [keep.tile([P, SLOTS], F32, name="y_rows%d" % j) for j in range(N_TILES)]

        def zero(engine, tile):
            engine.memset(tile[:].bitcast(I32), 0)

        def load_planes(tile, rows):
            planes = rows.shape[0]
            by_r = rows.bitcast(I32).rearrange("s (q r) c -> r q s c", r=4)
            for r in range(4):
                nc.sync.dma_start(tile[r:P:32, :].bitcast(I32).rearrange("q (s c) -> q s c", s=planes), by_r[r])

        def load_codes(tile, words):
            nc.sync.dma_start(tile[:].bitcast(I32).rearrange("p (s c) -> p s c", s=words.shape[0]), words.bitcast(I32).rearrange("s p c -> p s c"))

        w1_codes = {}

        def load_w1(e, passes, tag):
            tile = keep.tile([P, len(passes) * 2 * H], U8, name="w1_codes", tag=tag, align_bytes=64)
            load_codes(tile, w1_words[e, passes[0] : passes[-1] + 1])
            for i, a in enumerate(passes):
                w1_codes[e, a] = tile[:, i * 2 * H : (i + 1) * 2 * H]

        zero(nc.vector, x_scale_rows)
        zero(nc.vector, w1_planes[0])
        for group in shifted:
            for tile in group:
                zero(nc.gpsimd, tile)
        make_identity(nc, ident[:])

        nc.sync.dma_start(offs_t[:], offs)
        nc.sync.dma_start(pos1_t[:], pos1)
        nc.sync.dma_start(pos2_t[:], pos2)
        for q in range(4):
            nc.sync.dma_start(x_scale_rows[32 * q : 32 * q + 16, :].bitcast(I32), x_scales[:, 4 * q : 4 * q + 4, :].bitcast(I32))
        nc.sync.dma_start(
            x_codes[:].rearrange("p (a t) -> p a t", a=PASSES),
            x_words.rearrange("a p t r -> a p (t r)").bitcast(I32).rearrange("a p t -> p a t"),
        )
        load_w1(0, range(PASSES), "w1_first")
        load_planes(w1_planes[0], w1_scales[0:2].rearrange("e s f c -> (e s) f c"))

        def gather_scales(g):
            lo, hi = groups[g]
            for e in range(lo, hi):
                entries = offs_t[:, e * C // PER_COL : (e + 1) * C // PER_COL]
                nc.vector.tensor_copy(slot_scales[g][:, (e - lo) * C : (e - lo + 1) * C], x_scale_rows[:].indirect(entries))

        def shift_scales(g):
            for a in range(1, PASSES):
                nc.sync.dma_start(
                    shifted[g][a - 1][0:SHIFT_ROWS, :].bitcast(I32),
                    slot_scales[g][4 * a : 4 * a + SHIFT_ROWS, :].bitcast(I32),
                )

        def gather_words(e):
            entries = offs_t[:, e * C // PER_COL : (e + 1) * C // PER_COL]
            for a in range(PASSES):
                window = x_codes[:, a * T : (a + 1) * T].bitcast(U32)
                nc.vector.tensor_copy(slot_words[e][a][:], window.indirect(entries))

        def token_plane(e, a, b):
            g = min(e, 1)
            lo, hi = groups[g]
            first = (e - lo) * C + b * P
            if a == 0:
                return slot_scales[g][:, first : first + P]
            return shifted[g][a - 1][:, first : first + P]

        pre = {}

        def first_layer(e, blocks):
            for b in blocks:
                pre[e, b] = psum_a.tile([P, H], F32, name="acc")
            steps = [(a, b) for b in blocks for a in range(PASSES)]
            if e < 2:
                steps = sorted(steps)
            for a, b in steps:
                plane = ((e % 2) * PASSES + a) * H
                nc.tensor.matmul_mx(
                    out=pre[e, b][:],
                    lhsT=slot_words[e][a][:, b * P : (b + 1) * P].bitcast(FP8X4),
                    lhsT_scale=token_plane(e, a, b),
                    rhs=w1_codes[e, a].bitcast(FP4X4),
                    rhs_scale=w1_planes[e // 2][:, plane : plane + H],
                    start=(a == 0),
                    stop=(a == PASSES - 1),
                )

        def hidden(e):
            for b in range(BLOCKS):
                h_slots = ring.tile([P, H], BF16, name="h_slots")
                nc.scalar.activation(
                    h_slots[:].rearrange("s (u p d) -> s u p d", u=2, d=2),
                    pre[e, b][:].rearrange("s (p u d) -> s u p d", u=2, d=2),
                    GELU,
                )
                pairs = h_slots[:].bitcast(F32)
                turned = psum_t.tile([P, 2 * P], F32, name="turned")
                for u in range(2):
                    nc.tensor.transpose(turned[:, u * P : (u + 1) * P], pairs[:, u * P : (u + 1) * P], ident[:])
                h_grouped = ring.tile([P, 4 * P], BF16, name="h_grouped", align_bytes=64, bufs=E * BLOCKS)
                copy = nc.vector.tensor_copy if (e, b) == (E - 1, 0) else nc.scalar.copy
                copy(
                    h_grouped[:].bitcast(F32).rearrange("p (s u) -> p s u", u=2),
                    turned[:].rearrange("p (u s) -> p s u", u=2),
                )
                nc.vector.quantize_mx(
                    out=h_codes[e][:, b * P : (b + 1) * P].bitcast(FP8X4),
                    scales=h_scales[e][:, b * P : (b + 1) * P],
                    in_=h_grouped[:],
                )

        def second_layer(j, first_slot, n_slots, copy):
            sums = psum_y.tile([P, n_slots], F32, name="sums") if j < 2 else psum_a.tile([P, n_slots], F32, name="acc")
            width = min(C, n_slots)
            for i in range(0, n_slots, width):
                e, c = divmod(first_slot + i, C)
                col = e * N + j * P
                nc.tensor.matmul_mx(
                    out=sums[:, i : i + width],
                    lhsT=w2_codes[:, 2 * col : 2 * (col + P)].bitcast(FP4X4),
                    lhsT_scale=w2_planes[:, col : col + P],
                    rhs=h_codes[e][:, c : c + width].bitcast(FP8X4),
                    rhs_scale=h_scales[e][:, c : c + width],
                    start=True,
                    stop=True,
                )
            copy(y_rows[j][:, first_slot : first_slot + n_slots], sums[:])

        gather_scales(0)
        shift_scales(0)
        gather_scales(1)
        load_w1(1, range(PASSES), "early")
        shift_scales(1)
        gather_words(0)
        for e in range(E - 1):
            if e > 0:
                gather_words(e)
            first_layer(e, range(BLOCKS))
            if e == 0:
                load_w1(2, range(PASSES), "slot_words0_0")
                w1_planes.append(keep.tile([P, 2 * PASSES * H], U8, name="w1_planes_late", tag="slot_words0_1", align_bytes=64))
                zero(nc.gpsimd, w1_planes[1])
                load_planes(w1_planes[1], w1_scales[2:E].rearrange("e s f c -> (e s) f c"))
                load_w1(3, range(PASSES), "slot_words0_2")
                w2_codes = keep.tile([P, E * 2 * N], U8, name="w2_codes", tag="slot_words0_3", align_bytes=64)
                load_codes(w2_codes, w2_words.rearrange("e s p c -> (e s) p c"))
            if e == 1:
                w2_planes = keep.tile([P, E * N], U8, name="w2_planes", tag="slot_words1_0", align_bytes=64)
                zero(nc.gpsimd, w2_planes)
                load_planes(w2_planes, w2_scales.rearrange("e s f c -> (e s) f c"))
                gates = keep.tile([P, 2 * T], F32, name="gates", tag="slot_words1_3", align_bytes=64)
                nc.sync.dma_start(gates[:].rearrange("p (r t) -> p r t", r=2), gate[:, 0:P, :].rearrange("r p t -> p r t"))
            if e > 0:
                hidden(e - 1)
        gather_words(E - 1)
        first_layer(E - 1, [0])
        hidden(E - 2)
        second_layer(0, 0, 2 * C, nc.vector.tensor_copy)
        first_layer(E - 1, [1])
        second_layer(0, 2 * C, C, nc.vector.tensor_copy)
        hidden(E - 1)
        second_layer(0, 3 * C, P, nc.scalar.copy)
        second_layer(0, 3 * C + P, P, nc.scalar.copy)
        for j in range(1, N_TILES):
            second_layer(j, 0, 2 * C, nc.scalar.copy)
            second_layer(j, 2 * C, 2 * C, nc.scalar.copy)

        pieces = [(j, 0, T) for j in range(N_TILES - 1)] + [(N_TILES - 1, 0, T // 2), (N_TILES - 1, T // 2, T)]
        products = {}

        def product(piece, r):
            j, lo, hi = piece
            entries = (pos1_t, pos2_t)[r][:, lo // PER_COL : hi // PER_COL]
            products[piece, r] = ring.tile([P, hi - lo], F32, name="product%d" % r)
            nc.vector.tensor_tensor(products[piece, r][:], y_rows[j][:].indirect(entries), gates[:, r * T + lo : r * T + hi], MULT)

        def finish(piece):
            j, lo, hi = piece
            total = ring.tile([P, hi - lo], F32, name="total")
            if j >= 2:
                nc.vector.tensor_tensor(total[:], products[piece, 0][:], products[piece, 1][:], ADD)
            else:
                by_token = psum_a.tile([P, T], F32, name="acc")
                for c in range(0, T, P):
                    for r in range(2):
                        nc.tensor.matmul(by_token[:, c : c + P], lhsT=products[piece, r][:, c : c + P], rhs=ident[:], is_transpose=True, start=(r == 0), stop=(r == 1))
                staged = ring.tile([P, T], F32, name="staged")
                nc.scalar.copy(staged[:], by_token[:])
                by_row = psum_a.tile([P, T], F32, name="acc")
                for c in range(0, T, P):
                    nc.tensor.transpose(by_row[:, c : c + P], staged[:, c : c + P], ident[:])
                nc.scalar.copy(total[:], by_row[:])
            nc.sync.dma_start(out[j * P : (j + 1) * P, lo:hi], total[:])

        for i, piece in enumerate(pieces):
            product(piece, 0)
            if i > 0:
                finish(pieces[i - 1])
            product(piece, 1)
        finish(pieces[-1])
